import numpy as np, ml_dtypes
CORES = [76,84,92,100,108,116,124]
N = 7
import mx_ref
NC = 128
EPS = 0.001
BF = ml_dtypes.bfloat16
def setup_inputs(rng):
    def f(*shape):
        return mx_ref.flush((rng.standard_normal(shape, dtype=np.float32) * np.exp2(rng.integers(-2, 3, shape[:-1] + (1,)))).astype(BF))
    return {"x": f(N, 128, 512), "w": f(N, 128, 4 * NC)}
def setup_inputs_blocks(rng):
    d = setup_inputs(rng)
    for k in ("x", "w"): d[k] = mx_ref.spread(d[k], rng, 4)
    return d
def setup_inputs_wide(rng):
    d = setup_inputs(rng)
    for k in ("x", "w"): d[k] = mx_ref.flush((d[k].astype(np.float32) * np.exp2(rng.integers(-6, 7, (N, 1, 1))).astype(np.float32)).astype(BF))
    return d
def setup_inputs_tokens(rng):
    d = setup_inputs(rng); v = d["x"].astype(np.float32).reshape(N, 128, -1, 4)
    d["x"] = mx_ref.flush((v * np.exp2(rng.integers(-6, 7, (N, 1, v.shape[2], 1))).astype(np.float32)).reshape(d["x"].shape).astype(BF))
    return d
def setup_inputs_faint(rng):
    d = setup_inputs(rng); d["x"] = mx_ref.flush((d["x"].astype(np.float32) * np.float32(2.0 ** -12)).astype(BF))
    return d
def reference(x, w):
    W = [mx_ref.quantize(w[r]) for r in range(N)]
    y = np.zeros((N, 128, N * NC), np.float32)
    for j in range(N):
        X = mx_ref.quantize(x[j])
        Z = [mx_ref.matmul(X, W[r]) for r in range(N)]
        ms = sum((z.astype(np.float64) ** 2).sum(axis=1, keepdims=True) for z in Z) / (N * NC)
        for r in range(N):
            y[r][:, NC * j:NC * j + NC] = (Z[r] / np.sqrt(ms + EPS)).astype(np.float32)
    return {"y": y}

@@ -1,0 +1,265 @@
+from concourse.bass import DstId, RemoteDMATransfer
+from concourse.mybir import dt, AluOpType, AxisListType, ActivationFunctionType
+
+N = 7
+NC = 128
+EPS = 0.001
+SLOT = 2 * NC
+NB = 8
+NP = N // 2
+AW = 136
+SH = 2.0 ** -20
+NG = 2
+G1 = 4
+
+SCRATCH = {
+    "xt": ("sbuf", [128, 4 * NC], "bfloat16"),
+    "wt": ("sbuf", [128, 4 * NC], "bfloat16"),
+    "q": ("sbuf", [128, N * SLOT], "float8_e4m3fn_x4"),
+    "sc": ("sbuf", [128, N * SLOT], "uint8"),
+    "ps": ("psum", [128, 512 * NB], "float32"),
+    "junk": ("sbuf", [128, N * NP * SLOT], "float32"),
+    "tmp": ("sbuf", [128, N * NC], "float32"),
+    "z": ("sbuf", [128, N * NC], "float32"),
+    "acc": ("sbuf", [128, N * AW], "float32"),
+    "ss": ("sbuf", [128, 8], "float32"),
+    "rt": ("sbuf", [128, 8], "float32"),
+    "ri": ("sbuf", [128, 8], "float32"),
+}
+SEMAPHORES = (["lx", "lw", "qz", "rc", "rs", "ls", "vq", "st"]
+              + ["arr%d" % i for i in range(N)] + ["bk%d" % i for i in range(NB)] + ["yd%d" % i for i in range(N)]
+              + ["fs%d" % i for i in range(NG)] + ["fq%d" % i for i in range(NG)] + ["fr%d" % i for i in range(NG)])
+
+
+def _bits(mask):
+    return [1 << i for i in range(mask.bit_length()) if (mask >> i) & 1]
+
+
+def _join(bits):
+    m = 0
+    for b in bits:
+        m |= b
+    return m
+
+
+def _plan(cores, topo):
+    groups = []
+    for c in cores:
+        for grp in groups:
+            if topo.same_plane(topo.chip(c), topo.chip(grp[0])):
+                grp.append(c)
+                break
+        else:
+            groups.append([c])
+    groups.sort(key=lambda grp: -len(grp))
+    slots = [c for grp in groups for c in grp]
+    routes, when = {}, {}
+    for grp in groups:
+        for i, c in enumerate(grp):
+            same = grp[i + 1:] + grp[:i]
+            cross = [d for d in cores if d not in grp]
+            mate = [d for d in cross if topo.mates(topo.chip(c), topo.chip(d))]
+            far = [d for d in cross if d not in mate]
+            k = i % len(far)
+            far = far[k:] + far[:k]
+            helpers = [h for h in range(topo.CHIPS * topo.CORES_PER_CHIP)
+                       if topo.chip(h) == topo.chip(c) and h not in cores and all(topo.may_write(h, d) for d in cross)]
+            near = [h for h in helpers if topo.die(h) == topo.die(c)][0]
+            other = [h for h in helpers if topo.die(h) != topo.die(c)][0]
+            b, a = far[:2], mate + far[2:]
+            while len(a) < 2 and len(same) > 2:
+                a.append(same.pop())
+            routes[c] = (same, (near, a), (other, b))
+            when[(c, c)] = 0.0
+            for p, d in enumerate(same):
+                when[(c, d)] = 3.0 + p
+            for lst in (a, b):
+                for p, d in enumerate(lst):
+                    when[(c, d)] = 3.8 + p
+    return slots, routes, when
+
+
+def _views(T, slot):
+    lo, hi = slot * SLOT, (slot + 1) * SLOT
+    return T.q[:, lo:hi].bitcast(dt.uint8), T.sc[:, lo:hi]
+
+
+def _send(g, T, topo, core, slot, dests, tot, gate=None):
+    codes, plane = _views(T, slot)
+    for i, d in enumerate(dests):
+        rid, pid, _ = topo.addr(d)
+        m = topo.mask(core, d)
+        for k, v in enumerate((codes, plane)):
+            if gate is not None and i == 0:
+                g.wait_ge(T.sem[gate[k][0]], gate[k][1])
+            g.remote_dma(v, v, T.sem["arr%d" % slot], T.sem.ls, pid, rid, m)
+            tot["ls"] = tot.get("ls", 0) + len(_bits(m))
+
+
+def rank_program(g, core, T, topo):
+    cores = list(T.cores)
+    slots, routes, when = _plan(cores, topo)
+    tot = {}
+
+    def halves(src, a, b):
+        bits = _bits(topo.mask(src, a) & topo.mask(src, b))
+        h = len(bits) // 2
+        return _join(bits[h:]), _join(bits[:h])
+
+    if T.rank_of(core) is None:
+        for src in cores:
+            same, (near, a), (other, b) = routes[src]
+            if core in (near, other):
+                ma, mb = halves(src, near, other)
+                n = len(_bits(ma if core == near else mb))
+                _send(g, T, topo, core, slots.index(src), a if core == near else b, tot, gate=(("rc", n), ("rs", n)))
+                g.wait_ge(T.sem.ls, tot["ls"])
+        return
+
+    me = slots.index(core)
+    sem = T.sem
+
+    def inc(ins, name, n=1):
+        ins.then_inc(sem[name], n)
+        tot[name] = tot.get(name, 0) + n
+        return (name, tot[name])
+
+    def xcol(s):
+        return s * SLOT + (NC if s % 2 else 0)
+
+    def wcol(s):
+        return s * SLOT + (0 if s % 2 else NC)
+
+    inc(g.sync.dma_start(T.xt[:], T.x[:]), "lx", 16)
+    inc(g.scalar.dma_start(T.wt[:], T.w[:]), "lw", 16)
+    g.vector.wait_ge(sem.lx, 16)
+    inc(g.vector.quantize_mx(T.q[:, xcol(me):xcol(me) + NC], T.sc[:, xcol(me):xcol(me) + NC], T.xt[:]), "qz")
+    g.vector.wait_ge(sem.lw, 16)
+    inc(g.vector.quantize_mx(T.q[:, wcol(me):wcol(me) + NC], T.sc[:, wcol(me):wcol(me) + NC], T.wt[:]), "qz")
+
+    same, (near, a), (other, b) = routes[core]
+    ma, mb = halves(core, near, other)
+    g.wait_ge(sem.qz, 2)
+    for v, name in zip(_views(T, me), ("rc", "rs")):
+        trs = []
+        for h, m in ((near, ma), (other, mb)):
+            rid, pid, _ = topo.addr(h)
+            trs.append(RemoteDMATransfer(dst_ids=[DstId(rid=rid, pnc=pid)], dma_engine_mask=m, remote_sem=sem[name],
+                                         src=v, dst=v))
+            tot["ls"] = tot.get("ls", 0) + len(_bits(m))
+        g.remote_dma_fused(trs, local_sem=sem.ls)
+    _send(g, T, topo, core, me, same, tot)
+
+    for s, src in enumerate(slots):
+        if s != me:
+            snd = [x for x, lst in ((src, routes[src][0]), routes[src][1], routes[src][2]) if core in lst][0]
+            tot["arr%d" % s] = 2 * len(_bits(topo.mask(snd, core)))
+
+    by = sorted(range(N), key=lambda s: (when[(slots[s], core)], s))
+    idx = {s: i for i, s in enumerate(by)}
+
+    def members(p):
+        return [2 * p, 2 * p + 1] if p < NP else [N - 1]
+
+    units = [(j, p) for j in range(N) for p in range(NP + 1)]
+    units.sort(key=lambda u: (max(idx[s] for s in [u[0]] + members(u[1])), idx[u[0]], u[1]))
+    last = {}
+    for i, (j, p) in enumerate(units):
+        last[j] = i
+    done = sorted(range(N), key=lambda j: last[j])
+    pos = {j: k for k, j in enumerate(done)}
+    groups = [done[:G1], done[G1:]]
+
+    seen, dep, zdep, later = set(), {j: [] for j in range(N)}, {}, []
+    nsq = [0]
+
+    def zblk(j):
+        return T.z[:, j * NC:(j + 1) * NC]
+
+    def finish(k, at):
+        toks = groups[k]
+        lo, hi = pos[toks[0]], pos[toks[-1]] + 1
+
+        def sums():
+            for j in toks:
+                for name, n in dep[j]:
+                    g.vector.wait_ge(sem[name], n)
+                inc(g.vector.tensor_reduce(T.ss[:, pos[j]:pos[j] + 1], T.acc[:, j * AW:j * AW + NC + NP],
+                                           AxisListType.X, AluOpType.add), "fs%d" % k)
+
+        def root():
+            g.scalar.wait_ge(sem["fs%d" % k], len(toks))
+            inc(g.scalar.activation(T.rt[:, lo:hi], T.ss[:, lo:hi], ActivationFunctionType.Sqrt,
+                                    bias=EPS * SH * SH, scale=SH / (N * NC)), "fq%d" % k)
+
+        def recip():
+            g.vector.wait_ge(sem["fq%d" % k], 1)
+            inc(g.vector.reciprocal(T.ri[:, lo:hi], T.rt[:, lo:hi]), "fr%d" % k)
+
+        def scale(j, on_vector):
+            def f():
+                e = g.vector if on_vector else g.scalar
+                e.wait_ge(sem["fr%d" % k], 1)
+                e.wait_ge(sem[zdep[j][0]], zdep[j][1])
+                col = T.ri[:, pos[j]:pos[j] + 1]
+                if on_vector:
+                    ins = g.vector.tensor_scalar(zblk(j), zblk(j), col, None, AluOpType.mult)
+                else:
+                    ins = g.scalar.activation(zblk(j), zblk(j), ActivationFunctionType.Copy, scale=col)
+                inc(ins, "yd%d" % j)
+                r = T.rank_of(slots[j])
+                g.sync.wait_ge(sem["yd%d" % j], 1)
+                inc(g.sync.dma_start(T.y[:, r * NC:(r + 1) * NC], zblk(j)), "st", 16)
+            return f
+
+        later.append((at, sums))
+        later.append((at + 1, root))
+        later.append((at + 3, recip))
+        for n, j in enumerate(toks):
+            later.append((at + 4 + n // 2, scale(j, n % 2 == 0)))
+
+    for i, (j, p) in enumerate(units):
+        bank = "bk%d" % (i % NB)
+        n = SLOT if p < NP else NC
+        out = T.ps[:, (i % NB) * 512:(i % NB) * 512 + n]
+        for s in [j] + members(p):
+            if s not in seen:
+                seen.add(s)
+                if s == me:
+                    g.tensor.wait_ge(sem.qz, 2)
+                else:
+                    g.tensor.wait_ge(sem["arr%d" % s], tot["arr%d" % s])
+        if tot.get(bank, 0):
+            g.tensor.wait_ge(sem[bank], tot[bank])
+        xc, wc = xcol(j), wcol(members(p)[0])
+        inc(g.tensor.matmul_mx(out, T.q[:, xc:xc + NC], T.sc[:, xc:xc + NC], T.q[:, wc:wc + n], T.sc[:, wc:wc + n],
+                               True, True), bank)
+        if p < NP:
+            g.scalar.wait_ge(sem[bank], tot[bank])
+            k = nsq[0]
+            nsq[0] += 1
+            dep[j].append(inc(g.scalar.activation(T.junk[:, k * SLOT:(k + 1) * SLOT], out, ActivationFunctionType.Square,
+                                                  scale=SH ** 0.5, accum_out=T.acc[:, j * AW + NC + p:j * AW + NC + p + 1]),
+                              bank))
+            if me in members(p):
+                o = (i % NB) * 512 + members(p).index(me) * NC
+                g.vector.wait_ge(sem[bank], tot[bank])
+                zdep[j] = inc(g.vector.tensor_scalar(zblk(j), T.ps[:, o:o + NC], SH, None, AluOpType.mult), bank)
+        else:
+            keep = zblk(j) if me in members(p) else T.tmp[:, j * NC:(j + 1) * NC]
+            g.vector.wait_ge(sem[bank], tot[bank])
+            d = inc(g.vector.tensor_scalar(keep, out, SH, None, AluOpType.mult), "vq")
+            if me in members(p):
+                zdep[j] = d
+            g.vector.wait_ge(sem.vq, tot["vq"])
+            dep[j].append(inc(g.vector.tensor_tensor(T.acc[:, j * AW:j * AW + NC], out, keep, AluOpType.mult), bank))
+        for k, toks in enumerate(groups):
+            if last[toks[-1]] == i:
+                finish(k, i)
+        while later and later[0][0] <= i:
+            later.pop(0)[1]()
+    while later:
+        later.pop(0)[1]()
+
+    for name in sorted(tot, key=lambda s: s == "st"):
+        g.wait_ge(sem[name], tot[name])

@@ -4,31 +4,29 @@ from concourse.mybir import dt, AluOpType, AxisListType, ActivationFunctionType
 N = 7
 NC = 128
 EPS = 0.001
-SLOT = 2 * NC
-NB = 8
-NP = N // 2
-AW = 136
+BANK = 512
 SH = 2.0 ** -20
-NG = 2
-G1 = 4
+NV = 4
 
 SCRATCH = {
     "xt": ("sbuf", [128, 4 * NC], "bfloat16"),
     "wt": ("sbuf", [128, 4 * NC], "bfloat16"),
-    "q": ("sbuf", [128, N * SLOT], "float8_e4m3fn_x4"),
-    "sc": ("sbuf", [128, N * SLOT], "uint8"),
-    "ps": ("psum", [128, 512 * NB], "float32"),
-    "junk": ("sbuf", [128, N * NP * SLOT], "float32"),
-    "tmp": ("sbuf", [128, N * NC], "float32"),
-    "z": ("sbuf", [128, N * NC], "float32"),
-    "acc": ("sbuf", [128, N * AW], "float32"),
-    "ss": ("sbuf", [128, 8], "float32"),
+    "q": ("sbuf", [128, N * NC], "float8_e4m3fn_x4"),
+    "sc": ("sbuf", [128, N * NC], "uint8"),
+    "wq": ("sbuf", [128, NC], "float8_e4m3fn_x4"),
+    "ws": ("sbuf", [128, NC], "uint8"),
+    "ps": ("psum", [128, BANK * N], "float32"),
+    "junk": ("sbuf", [128, N * NC], "float32"),
+    "pa": ("sbuf", [128, 8], "float32"),
+    "pd": ("dram", [N, 128, N], "float32"),
+    "tot": ("sbuf", [128, 8], "float32"),
     "rt": ("sbuf", [128, 8], "float32"),
+    "r0": ("sbuf", [128, 8], "float32"),
     "ri": ("sbuf", [128, 8], "float32"),
+    "yt": ("sbuf", [128, N * NC], "float32"),
 }
-SEMAPHORES = (["lx", "lw", "qz", "rc", "rs", "ls", "vq", "st"]
-              + ["arr%d" % i for i in range(N)] + ["bk%d" % i for i in range(NB)] + ["yd%d" % i for i in range(N)]
-              + ["fs%d" % i for i in range(NG)] + ["fq%d" % i for i in range(NG)] + ["fr%d" % i for i in range(NG)])
+SEMAPHORES = (["lx", "lw", "qx", "qw", "rc", "rs", "ls", "sq", "po", "pq", "tt", "fq", "fr", "fi", "yv", "ys", "st"]
+              + ["arr%d" % i for i in range(N)] + ["mm%d" % i for i in range(N)])
 
 
 def _bits(mask):
@@ -52,7 +50,8 @@ def _plan(cores, topo):
         else:
             groups.append([c])
     groups.sort(key=lambda grp: -len(grp))
-    slots = [c for grp in groups for c in grp]
+    everyone = range(topo.CHIPS * topo.CORES_PER_CHIP)
+    homes = [topo.chip(c) for c in cores]
     routes, when = {}, {}
     for grp in groups:
         for i, c in enumerate(grp):
@@ -62,8 +61,9 @@ def _plan(cores, topo):
             far = [d for d in cross if d not in mate]
             k = i % len(far)
             far = far[k:] + far[:k]
-            helpers = [h for h in range(topo.CHIPS * topo.CORES_PER_CHIP)
-                       if topo.chip(h) == topo.chip(c) and h not in cores and all(topo.may_write(h, d) for d in cross)]
+            helpers = [h for h in everyone
+                       if topo.chip(h) == topo.chip(c) and h not in cores
+                       and all(topo.may_write(h, e) for e in everyone if topo.chip(e) in homes and e != h)]
             near = [h for h in helpers if topo.die(h) == topo.die(c)][0]
             other = [h for h in helpers if topo.die(h) != topo.die(c)][0]
             b, a = far[:2], mate + far[2:]
@@ -76,11 +76,11 @@ def _plan(cores, topo):
             for lst in (a, b):
                 for p, d in enumerate(lst):
                     when[(c, d)] = 3.8 + p
-    return slots, routes, when
+    return routes, when
 
 
 def _views(T, slot):
-    lo, hi = slot * SLOT, (slot + 1) * SLOT
+    lo, hi = slot * NC, (slot + 1) * NC
     return T.q[:, lo:hi].bitcast(dt.uint8), T.sc[:, lo:hi]
 
 
@@ -98,7 +98,9 @@ def _send(g, T, topo, core, slot, dests, tot, gate=None):
 
 def rank_program(g, core, T, topo):
     cores = list(T.cores)
-    slots, routes, when = _plan(cores, topo)
+    routes, when = _plan(cores, topo)
+    hub = {c: routes[c][1][0] for c in cores}
+    sem = T.sem
     tot = {}
 
     def halves(src, a, b):
@@ -106,40 +108,65 @@ def rank_program(g, core, T, topo):
         h = len(bits) // 2
         return _join(bits[h:]), _join(bits[:h])
 
+    def fold_mask(src):
+        far = [hub[d] for d in cores if d != src][0]
+        return topo.mask(hub[src], src) & topo.mask(hub[src], far)
+
     if T.rank_of(core) is None:
         for src in cores:
             same, (near, a), (other, b) = routes[src]
-            if core in (near, other):
-                ma, mb = halves(src, near, other)
-                n = len(_bits(ma if core == near else mb))
-                _send(g, T, topo, core, slots.index(src), a if core == near else b, tot, gate=(("rc", n), ("rs", n)))
-                g.wait_ge(T.sem.ls, tot["ls"])
+            if core not in (near, other):
+                continue
+            r = cores.index(src)
+            ma, mb = halves(src, near, other)
+            n = len(_bits(ma if core == near else mb))
+            _send(g, T, topo, core, r, a if core == near else b, tot, gate=(("rc", n), ("rs", n)))
+            if core == hub[src]:
+                g.wait_ge(sem.po, len(_bits(topo.mask(src, core))))
+                others = [hub[d] for d in cores if d != src]
+                trs = []
+                for i, h in enumerate(others):
+                    rid, pid, _ = topo.addr(h)
+                    trs.append(RemoteDMATransfer(dst_ids=[DstId(rid=rid, pnc=pid)],
+                                                 dma_engine_mask=_bits(topo.mask(core, h))[i], remote_sem=sem.pq,
+                                                 src=T.pd[r], dst=T.pd[r]))
+                    tot["ls"] += 1
+                g.remote_dma_fused(trs, local_sem=sem.ls)
+                g.wait_ge(sem.pq, len(others))
+                rid, pid, _ = topo.addr(src)
+                m = fold_mask(src)
+                g.remote_dma_fused([RemoteDMATransfer(dst_ids=[DstId(rid=rid, pnc=pid)], dma_engine_mask=m,
+                                                      remote_sem=sem.tt, srcs=[T.pd[k] for k in range(N)],
+                                                      dsts=[T.tot[:, 0:N]], alu_op=1)], local_sem=sem.ls)
+                tot["ls"] += len(_bits(m))
+            g.wait_ge(sem.ls, tot["ls"])
         return
 
-    me = slots.index(core)
-    sem = T.sem
+    me = cores.index(core)
 
     def inc(ins, name, n=1):
         ins.then_inc(sem[name], n)
         tot[name] = tot.get(name, 0) + n
-        return (name, tot[name])
 
-    def xcol(s):
-        return s * SLOT + (NC if s % 2 else 0)
+    def xq(s):
+        return T.q[:, s * NC:(s + 1) * NC], T.sc[:, s * NC:(s + 1) * NC]
 
-    def wcol(s):
-        return s * SLOT + (0 if s % 2 else NC)
+    def bank(s):
+        return T.ps[:, s * BANK:s * BANK + NC]
+
+    def yblk(s):
+        return T.yt[:, s * NC:(s + 1) * NC]
 
     inc(g.sync.dma_start(T.xt[:], T.x[:]), "lx", 16)
-    inc(g.scalar.dma_start(T.wt[:], T.w[:]), "lw", 16)
+    inc(g.sync.dma_start(T.wt[:], T.w[:]), "lw", 16)
     g.vector.wait_ge(sem.lx, 16)
-    inc(g.vector.quantize_mx(T.q[:, xcol(me):xcol(me) + NC], T.sc[:, xcol(me):xcol(me) + NC], T.xt[:]), "qz")
+    inc(g.vector.quantize_mx(xq(me)[0], xq(me)[1], T.xt[:]), "qx")
     g.vector.wait_ge(sem.lw, 16)
-    inc(g.vector.quantize_mx(T.q[:, wcol(me):wcol(me) + NC], T.sc[:, wcol(me):wcol(me) + NC], T.wt[:]), "qz")
+    inc(g.vector.quantize_mx(T.wq[:], T.ws[:], T.wt[:]), "qw")
 
     same, (near, a), (other, b) = routes[core]
     ma, mb = halves(core, near, other)
-    g.wait_ge(sem.qz, 2)
+    g.wait_ge(sem.qx, 1)
     for v, name in zip(_views(T, me), ("rc", "rs")):
         trs = []
         for h, m in ((near, ma), (other, mb)):
@@ -150,116 +177,47 @@ def rank_program(g, core, T, topo):
         g.remote_dma_fused(trs, local_sem=sem.ls)
     _send(g, T, topo, core, me, same, tot)
 
-    for s, src in enumerate(slots):
+    for s, src in enumerate(cores):
         if s != me:
             snd = [x for x, lst in ((src, routes[src][0]), routes[src][1], routes[src][2]) if core in lst][0]
             tot["arr%d" % s] = 2 * len(_bits(topo.mask(snd, core)))
 
-    by = sorted(range(N), key=lambda s: (when[(slots[s], core)], s))
-    idx = {s: i for i, s in enumerate(by)}
-
-    def members(p):
-        return [2 * p, 2 * p + 1] if p < NP else [N - 1]
-
-    units = [(j, p) for j in range(N) for p in range(NP + 1)]
-    units.sort(key=lambda u: (max(idx[s] for s in [u[0]] + members(u[1])), idx[u[0]], u[1]))
-    last = {}
-    for i, (j, p) in enumerate(units):
-        last[j] = i
-    done = sorted(range(N), key=lambda j: last[j])
-    pos = {j: k for k, j in enumerate(done)}
-    groups = [done[:G1], done[G1:]]
-
-    seen, dep, zdep, later = set(), {j: [] for j in range(N)}, {}, []
-    nsq = [0]
-
-    def zblk(j):
-        return T.z[:, j * NC:(j + 1) * NC]
-
-    def finish(k, at):
-        toks = groups[k]
-        lo, hi = pos[toks[0]], pos[toks[-1]] + 1
-
-        def sums():
-            for j in toks:
-                for name, n in dep[j]:
-                    g.vector.wait_ge(sem[name], n)
-                inc(g.vector.tensor_reduce(T.ss[:, pos[j]:pos[j] + 1], T.acc[:, j * AW:j * AW + NC + NP],
-                                           AxisListType.X, AluOpType.add), "fs%d" % k)
-
-        def root():
-            g.scalar.wait_ge(sem["fs%d" % k], len(toks))
-            inc(g.scalar.activation(T.rt[:, lo:hi], T.ss[:, lo:hi], ActivationFunctionType.Sqrt,
-                                    bias=EPS * SH * SH, scale=SH / (N * NC)), "fq%d" % k)
-
-        def recip():
-            g.vector.wait_ge(sem["fq%d" % k], 1)
-            inc(g.vector.reciprocal(T.ri[:, lo:hi], T.rt[:, lo:hi]), "fr%d" % k)
-
-        def scale(j, on_vector):
-            def f():
-                e = g.vector if on_vector else g.scalar
-                e.wait_ge(sem["fr%d" % k], 1)
-                e.wait_ge(sem[zdep[j][0]], zdep[j][1])
-                col = T.ri[:, pos[j]:pos[j] + 1]
-                if on_vector:
-                    ins = g.vector.tensor_scalar(zblk(j), zblk(j), col, None, AluOpType.mult)
-                else:
-                    ins = g.scalar.activation(zblk(j), zblk(j), ActivationFunctionType.Copy, scale=col)
-                inc(ins, "yd%d" % j)
-                r = T.rank_of(slots[j])
-                g.sync.wait_ge(sem["yd%d" % j], 1)
-                inc(g.sync.dma_start(T.y[:, r * NC:(r + 1) * NC], zblk(j)), "st", 16)
-            return f
-
-        later.append((at, sums))
-        later.append((at + 1, root))
-        later.append((at + 3, recip))
-        for n, j in enumerate(toks):
-            later.append((at + 4 + n // 2, scale(j, n % 2 == 0)))
-
-    for i, (j, p) in enumerate(units):
-        bank = "bk%d" % (i % NB)
-        n = SLOT if p < NP else NC
-        out = T.ps[:, (i % NB) * 512:(i % NB) * 512 + n]
-        for s in [j] + members(p):
-            if s not in seen:
-                seen.add(s)
-                if s == me:
-                    g.tensor.wait_ge(sem.qz, 2)
-                else:
-                    g.tensor.wait_ge(sem["arr%d" % s], tot["arr%d" % s])
-        if tot.get(bank, 0):
-            g.tensor.wait_ge(sem[bank], tot[bank])
-        xc, wc = xcol(j), wcol(members(p)[0])
-        inc(g.tensor.matmul_mx(out, T.q[:, xc:xc + NC], T.sc[:, xc:xc + NC], T.q[:, wc:wc + n], T.sc[:, wc:wc + n],
-                               True, True), bank)
-        if p < NP:
-            g.scalar.wait_ge(sem[bank], tot[bank])
-            k = nsq[0]
-            nsq[0] += 1
-            dep[j].append(inc(g.scalar.activation(T.junk[:, k * SLOT:(k + 1) * SLOT], out, ActivationFunctionType.Square,
-                                                  scale=SH ** 0.5, accum_out=T.acc[:, j * AW + NC + p:j * AW + NC + p + 1]),
-                              bank))
-            if me in members(p):
-                o = (i % NB) * 512 + members(p).index(me) * NC
-                g.vector.wait_ge(sem[bank], tot[bank])
-                zdep[j] = inc(g.vector.tensor_scalar(zblk(j), T.ps[:, o:o + NC], SH, None, AluOpType.mult), bank)
+    g.tensor.wait_ge(sem.qw, 1)
+    for s in sorted(range(N), key=lambda s: (when[(cores[s], core)], s)):
+        if s == me:
+            g.tensor.wait_ge(sem.qx, 1)
         else:
-            keep = zblk(j) if me in members(p) else T.tmp[:, j * NC:(j + 1) * NC]
-            g.vector.wait_ge(sem[bank], tot[bank])
-            d = inc(g.vector.tensor_scalar(keep, out, SH, None, AluOpType.mult), "vq")
-            if me in members(p):
-                zdep[j] = d
-            g.vector.wait_ge(sem.vq, tot["vq"])
-            dep[j].append(inc(g.vector.tensor_tensor(T.acc[:, j * AW:j * AW + NC], out, keep, AluOpType.mult), bank))
-        for k, toks in enumerate(groups):
-            if last[toks[-1]] == i:
-                finish(k, i)
-        while later and later[0][0] <= i:
-            later.pop(0)[1]()
-    while later:
-        later.pop(0)[1]()
+            g.tensor.wait_ge(sem["arr%d" % s], tot["arr%d" % s])
+        inc(g.tensor.matmul_mx(bank(s), xq(s)[0], xq(s)[1], T.wq[:], T.ws[:], True, True), "mm%d" % s)
+        g.scalar.wait_ge(sem["mm%d" % s], 1)
+        inc(g.scalar.activation(T.junk[:, s * NC:(s + 1) * NC], bank(s), ActivationFunctionType.Square,
+                                scale=SH ** 0.5, accum_out=T.pa[:, s:s + 1]), "sq")
+
+    g.wait_ge(sem.sq, N)
+    rid, pid, _ = topo.addr(hub[core])
+    m = topo.mask(core, hub[core])
+    g.remote_dma(T.pd[me], T.pa[:, 0:N], sem.po, sem.ls, pid, rid, m)
+    tot["ls"] += len(_bits(m))
+    tot["tt"] = len(_bits(fold_mask(core)))
+
+    g.scalar.wait_ge(sem.tt, tot["tt"])
+    inc(g.scalar.activation(T.rt[:, 0:N], T.tot[:, 0:N], ActivationFunctionType.Sqrt,
+                            bias=EPS * SH * SH, scale=SH / (N * NC)), "fq")
+    g.vector.wait_ge(sem.fq, 1)
+    inc(g.vector.reciprocal(T.r0[:, 0:N], T.rt[:, 0:N]), "fr")
+    g.vector.wait_ge(sem.fr, 1)
+    inc(g.vector.tensor_scalar(T.ri[:, 0:N], T.r0[:, 0:N], SH, None, AluOpType.mult), "fi")
+    g.vector.wait_ge(sem.fi, 1)
+    g.vector.wait_ge(sem.sq, N)
+    for j in range(NV):
+        inc(g.vector.tensor_scalar(yblk(j), bank(j), T.ri[:, j:j + 1], None, AluOpType.mult), "yv")
+    g.scalar.wait_ge(sem.fi, 1)
+    for j in range(NV, N):
+        inc(g.scalar.activation(yblk(j), bank(j), ActivationFunctionType.Copy, scale=T.ri[:, j:j + 1]), "ys")
+    g.sync.wait_ge(sem.yv, NV)
+    inc(g.sync.dma_start(T.y[:, 0:NV * NC], T.yt[:, 0:NV * NC]), "st", 16)
+    g.scalar.wait_ge(sem.ys, N - NV)
+    inc(g.scalar.dma_start(T.y[:, NV * NC:N * NC], T.yt[:, NV * NC:N * NC]), "st", 16)
 
     for name in sorted(tot, key=lambda s: s == "st"):
         g.wait_ge(sem[name], tot[name])

@@ -7,6 +7,9 @@ EPS = 0.001
 BANK = 512
 SH = 2.0 ** -20
 NV = 4
+KA = SH / (N * NC)
+E = EPS * SH * N * NC
+SU = 2.0 ** -50
 
 SCRATCH = {
     "xt": ("sbuf", [128, 4 * NC], "bfloat16"),
@@ -20,12 +23,19 @@ SCRATCH = {
     "pa": ("sbuf", [128, 8], "float32"),
     "pd": ("dram", [N, 128, N], "float32"),
     "tot": ("sbuf", [128, 8], "float32"),
-    "rt": ("sbuf", [128, 8], "float32"),
+    "a0": ("sbuf", [128, 8], "float32"),
+    "sa": ("sbuf", [128, 8], "float32"),
+    "ra": ("sbuf", [128, 8], "float32"),
+    "ca": ("sbuf", [128, 8], "float32"),
+    "cc": ("sbuf", [128, 8], "float32"),
+    "uu": ("sbuf", [128, 8], "float32"),
+    "su": ("sbuf", [128, 8], "float32"),
     "r0": ("sbuf", [128, 8], "float32"),
     "ri": ("sbuf", [128, 8], "float32"),
     "yt": ("sbuf", [128, N * NC], "float32"),
 }
-SEMAPHORES = (["lx", "lw", "qx", "qw", "rc", "rs", "ls", "sq", "po", "pq", "tt", "fq", "fr", "fi", "yv", "ys", "st"]
+SEMAPHORES = (["lx", "lw", "qx", "qw", "rc", "rs", "ls", "sq", "so", "se", "e1", "e2", "e3", "e4", "e5", "l1",
+               "po", "pq", "tt", "fq", "fr", "fi", "yv", "ys", "st"]
               + ["arr%d" % i for i in range(N)] + ["mm%d" % i for i in range(N)])
 
 
@@ -84,16 +94,33 @@ def _views(T, slot):
     return T.q[:, lo:hi].bitcast(dt.uint8), T.sc[:, lo:hi]
 
 
+def _common(topo, core, dests):
+    m = topo.mask(core, dests[0])
+    for d in dests[1:]:
+        m &= topo.mask(core, d)
+    return m
+
+
 def _send(g, T, topo, core, slot, dests, tot, gate=None):
     codes, plane = _views(T, slot)
+    bits = _bits(_common(topo, core, dests))
+    k = len(bits) // len(dests)
+    if gate is not None:
+        g.wait_ge(T.sem[gate[0][0]], gate[0][1])
+    trs = []
     for i, d in enumerate(dests):
         rid, pid, _ = topo.addr(d)
+        trs.append(RemoteDMATransfer(dst_ids=[DstId(rid=rid, pnc=pid)], dma_engine_mask=_join(bits[i * k:(i + 1) * k]),
+                                     remote_sem=T.sem["arr%d" % slot], src=plane, dst=plane))
+        tot["ls"] = tot.get("ls", 0) + k
+    g.remote_dma_fused(trs, local_sem=T.sem.ls)
+    if gate is not None:
+        g.wait_ge(T.sem[gate[1][0]], gate[1][1])
+    for d in dests:
+        rid, pid, _ = topo.addr(d)
         m = topo.mask(core, d)
-        for k, v in enumerate((codes, plane)):
-            if gate is not None and i == 0:
-                g.wait_ge(T.sem[gate[k][0]], gate[k][1])
-            g.remote_dma(v, v, T.sem["arr%d" % slot], T.sem.ls, pid, rid, m)
-            tot["ls"] = tot.get("ls", 0) + len(_bits(m))
+        g.remote_dma(codes, codes, T.sem["arr%d" % slot], T.sem.ls, pid, rid, m)
+        tot["ls"] += len(_bits(m))
 
 
 def rank_program(g, core, T, topo):
@@ -120,7 +147,7 @@ def rank_program(g, core, T, topo):
             r = cores.index(src)
             ma, mb = halves(src, near, other)
             n = len(_bits(ma if core == near else mb))
-            _send(g, T, topo, core, r, a if core == near else b, tot, gate=(("rc", n), ("rs", n)))
+            _send(g, T, topo, core, r, a if core == near else b, tot, gate=(("rs", n), ("rc", n)))
             if core == hub[src]:
                 g.wait_ge(sem.po, len(_bits(topo.mask(src, core))))
                 others = [hub[d] for d in cores if d != src]
@@ -166,8 +193,9 @@ def rank_program(g, core, T, topo):
 
     same, (near, a), (other, b) = routes[core]
     ma, mb = halves(core, near, other)
+    codes, plane = _views(T, me)
     g.wait_ge(sem.qx, 1)
-    for v, name in zip(_views(T, me), ("rc", "rs")):
+    for v, name in ((plane, "rs"), (codes, "rc")):
         trs = []
         for h, m in ((near, ma), (other, mb)):
             rid, pid, _ = topo.addr(h)
@@ -179,38 +207,58 @@ def rank_program(g, core, T, topo):
 
     for s, src in enumerate(cores):
         if s != me:
-            snd = [x for x, lst in ((src, routes[src][0]), routes[src][1], routes[src][2]) if core in lst][0]
-            tot["arr%d" % s] = 2 * len(_bits(topo.mask(snd, core)))
+            snd, lst = [(x, lst) for x, lst in ((src, routes[src][0]), routes[src][1], routes[src][2]) if core in lst][0]
+            tot["arr%d" % s] = len(_bits(_common(topo, snd, lst))) // len(lst) + len(_bits(topo.mask(snd, core)))
 
     g.tensor.wait_ge(sem.qw, 1)
     for s in sorted(range(N), key=lambda s: (when[(cores[s], core)], s)):
-        if s == me:
+        own = s == me
+        if own:
             g.tensor.wait_ge(sem.qx, 1)
         else:
             g.tensor.wait_ge(sem["arr%d" % s], tot["arr%d" % s])
         inc(g.tensor.matmul_mx(bank(s), xq(s)[0], xq(s)[1], T.wq[:], T.ws[:], True, True), "mm%d" % s)
         g.scalar.wait_ge(sem["mm%d" % s], 1)
         inc(g.scalar.activation(T.junk[:, s * NC:(s + 1) * NC], bank(s), ActivationFunctionType.Square,
-                                scale=SH ** 0.5, accum_out=T.pa[:, s:s + 1]), "sq")
+                                scale=SH ** 0.5, accum_out=T.pa[:, N:N + 1] if own else T.pa[:, s:s + 1]),
+            "so" if own else "sq")
+        if own:
+            g.vector.wait_ge(sem.so, 1)
+            inc(g.vector.tensor_scalar(T.pa[:, me:me + 1], T.pa[:, N:N + 1], E, None, AluOpType.add), "se")
 
-    g.wait_ge(sem.sq, N)
+    g.wait_ge(sem.sq, N - 1)
+    g.wait_ge(sem.se, 1)
     rid, pid, _ = topo.addr(hub[core])
     m = topo.mask(core, hub[core])
     g.remote_dma(T.pd[me], T.pa[:, 0:N], sem.po, sem.ls, pid, rid, m)
     tot["ls"] += len(_bits(m))
     tot["tt"] = len(_bits(fold_mask(core)))
 
-    g.scalar.wait_ge(sem.tt, tot["tt"])
-    inc(g.scalar.activation(T.rt[:, 0:N], T.tot[:, 0:N], ActivationFunctionType.Sqrt,
-                            bias=EPS * SH * SH, scale=SH / (N * NC)), "fq")
+    g.vector.wait_ge(sem.sq, N - 1)
+    g.vector.wait_ge(sem.se, 1)
+    inc(g.vector.tensor_scalar(T.a0[:, 0:N], T.pa[:, 0:N], E, None, AluOpType.add), "e1")
+    g.scalar.wait_ge(sem.e1, 1)
+    inc(g.scalar.activation(T.sa[:, 0:N], T.a0[:, 0:N], ActivationFunctionType.Sqrt, scale=KA), "e2")
+    g.vector.wait_ge(sem.e1, 1)
+    inc(g.vector.reciprocal(T.ra[:, 0:N], T.a0[:, 0:N]), "e3")
+    g.vector.wait_ge(sem.e2, 1)
+    inc(g.vector.reciprocal(T.ca[:, 0:N], T.sa[:, 0:N]), "e4")
+    g.vector.wait_ge(sem.e4, 1)
+    inc(g.vector.tensor_scalar(T.cc[:, 0:N], T.ca[:, 0:N], SH * SU ** 0.5, None, AluOpType.mult), "e5")
+
+    g.vector.wait_ge(sem.e3, 1)
+    g.vector.wait_ge(sem.e5, 1)
+    g.vector.wait_ge(sem.tt, tot["tt"])
+    inc(g.vector.tensor_tensor(T.uu[:, 0:N], T.tot[:, 0:N], T.ra[:, 0:N], AluOpType.mult), "l1")
+    g.scalar.wait_ge(sem.l1, 1)
+    inc(g.scalar.activation(T.su[:, 0:N], T.uu[:, 0:N], ActivationFunctionType.Sqrt, scale=SU), "fq")
     g.vector.wait_ge(sem.fq, 1)
-    inc(g.vector.reciprocal(T.r0[:, 0:N], T.rt[:, 0:N]), "fr")
+    inc(g.vector.reciprocal(T.r0[:, 0:N], T.su[:, 0:N]), "fr")
     g.vector.wait_ge(sem.fr, 1)
-    inc(g.vector.tensor_scalar(T.ri[:, 0:N], T.r0[:, 0:N], SH, None, AluOpType.mult), "fi")
-    g.vector.wait_ge(sem.fi, 1)
-    g.vector.wait_ge(sem.sq, N)
+    inc(g.vector.tensor_tensor(T.ri[:, NV:N], T.r0[:, NV:N], T.cc[:, NV:N], AluOpType.mult), "fi")
     for j in range(NV):
-        inc(g.vector.tensor_scalar(yblk(j), bank(j), T.ri[:, j:j + 1], None, AluOpType.mult), "yv")
+        inc(g.vector.tensor_scalar(yblk(j), bank(j), T.r0[:, j:j + 1], T.cc[:, j:j + 1], AluOpType.mult, AluOpType.mult),
+            "yv")
     g.scalar.wait_ge(sem.fi, 1)
     for j in range(NV, N):
         inc(g.scalar.activation(yblk(j), bank(j), ActivationFunctionType.Copy, scale=T.ri[:, j:j + 1]), "ys")

@@ -21,7 +21,9 @@ SCRATCH = {
     "ps": ("psum", [128, BANK * N], "float32"),
     "junk": ("sbuf", [128, N * NC], "float32"),
     "pa": ("sbuf", [128, 8], "float32"),
-    "pd": ("dram", [N, 128, N], "float32"),
+    "sl": ("sbuf", [128, (N - 1) * N], "float32"),
+    "sb": ("sbuf", [128, 4 * N], "float32"),
+    "sd": ("sbuf", [128, 2 * N], "float32"),
     "tot": ("sbuf", [128, 8], "float32"),
     "a0": ("sbuf", [128, 8], "float32"),
     "sa": ("sbuf", [128, 8], "float32"),
@@ -34,9 +36,9 @@ SCRATCH = {
     "ri": ("sbuf", [128, 8], "float32"),
     "yt": ("sbuf", [128, N * NC], "float32"),
 }
-SEMAPHORES = (["lx", "lw", "qx", "qw", "rc", "rs", "ls", "sq", "so", "se", "e1", "e2", "e3", "e4", "e5", "l1",
-               "po", "pq", "tt", "fq", "fr", "fi", "yv", "ys", "st"]
-              + ["arr%d" % i for i in range(N)] + ["mm%d" % i for i in range(N)])
+SEMAPHORES = (["lx", "lw", "qx", "qw", "rc", "rs", "wa", "ls", "sq", "so", "se", "ms", "e1", "e2", "e3", "e4", "e5",
+               "a1", "a2", "a3", "l1", "tt", "fq", "fr", "fi", "yv0", "yv1", "ys0", "ys1", "st"]
+              + ["arr%d" % i for i in range(N)] + ["fw%d" % i for i in range(N)] + ["mm%d" % i for i in range(N)])
 
 
 def _bits(mask):
@@ -70,22 +72,21 @@ def _plan(cores, topo):
             mate = [d for d in cross if topo.mates(topo.chip(c), topo.chip(d))]
             far = [d for d in cross if d not in mate]
             k = i % len(far)
-            far = far[k:] + far[:k]
+            jobs = far[k:] + far[:k] + mate
             helpers = [h for h in everyone
                        if topo.chip(h) == topo.chip(c) and h not in cores
                        and all(topo.may_write(h, e) for e in everyone if topo.chip(e) in homes and e != h)]
-            near = [h for h in helpers if topo.die(h) == topo.die(c)][0]
-            other = [h for h in helpers if topo.die(h) != topo.die(c)][0]
-            b, a = far[:2], mate + far[2:]
-            while len(a) < 2 and len(same) > 2:
-                a.append(same.pop())
-            routes[c] = (same, (near, a), (other, b))
+            near = [h for h in helpers if topo.die(h) == topo.die(c)]
+            other = [h for h in helpers if topo.die(h) != topo.die(c)]
+            relays = [near[0], other[0], near[1], other[1]]
+            while len(jobs) < len(relays) and len(same) > 2:
+                jobs.append(same.pop())
+            routes[c] = (same, [(h, [d]) for h, d in zip(relays, jobs)])
             when[(c, c)] = 0.0
             for p, d in enumerate(same):
                 when[(c, d)] = 3.0 + p
-            for lst in (a, b):
-                for p, d in enumerate(lst):
-                    when[(c, d)] = 3.8 + p
+            for d in jobs:
+                when[(c, d)] = 3.5
     return routes, when
 
 
@@ -126,50 +127,9 @@ def _send(g, T, topo, core, slot, dests, tot, gate=None):
 def rank_program(g, core, T, topo):
     cores = list(T.cores)
     routes, when = _plan(cores, topo)
-    hub = {c: routes[c][1][0] for c in cores}
+    hub = {c: routes[c][1][0][0] for c in cores}
     sem = T.sem
     tot = {}
-
-    def halves(src, a, b):
-        bits = _bits(topo.mask(src, a) & topo.mask(src, b))
-        h = len(bits) // 2
-        return _join(bits[h:]), _join(bits[:h])
-
-    def fold_mask(src):
-        far = [hub[d] for d in cores if d != src][0]
-        return topo.mask(hub[src], src) & topo.mask(hub[src], far)
-
-    if T.rank_of(core) is None:
-        for src in cores:
-            same, (near, a), (other, b) = routes[src]
-            if core not in (near, other):
-                continue
-            r = cores.index(src)
-            ma, mb = halves(src, near, other)
-            n = len(_bits(ma if core == near else mb))
-            _send(g, T, topo, core, r, a if core == near else b, tot, gate=(("rs", n), ("rc", n)))
-            if core == hub[src]:
-                g.wait_ge(sem.po, len(_bits(topo.mask(src, core))))
-                others = [hub[d] for d in cores if d != src]
-                trs = []
-                for i, h in enumerate(others):
-                    rid, pid, _ = topo.addr(h)
-                    trs.append(RemoteDMATransfer(dst_ids=[DstId(rid=rid, pnc=pid)],
-                                                 dma_engine_mask=_bits(topo.mask(core, h))[i], remote_sem=sem.pq,
-                                                 src=T.pd[r], dst=T.pd[r]))
-                    tot["ls"] += 1
-                g.remote_dma_fused(trs, local_sem=sem.ls)
-                g.wait_ge(sem.pq, len(others))
-                rid, pid, _ = topo.addr(src)
-                m = fold_mask(src)
-                g.remote_dma_fused([RemoteDMATransfer(dst_ids=[DstId(rid=rid, pnc=pid)], dma_engine_mask=m,
-                                                      remote_sem=sem.tt, srcs=[T.pd[k] for k in range(N)],
-                                                      dsts=[T.tot[:, 0:N]], alu_op=1)], local_sem=sem.ls)
-                tot["ls"] += len(_bits(m))
-            g.wait_ge(sem.ls, tot["ls"])
-        return
-
-    me = cores.index(core)
 
     def inc(ins, name, n=1):
         ins.then_inc(sem[name], n)
@@ -184,6 +144,112 @@ def rank_program(g, core, T, topo):
     def yblk(s):
         return T.yt[:, s * NC:(s + 1) * NC]
 
+    def deal(c):
+        rel = [h for h, _ in routes[c][1]]
+        bits = _bits(_common(topo, c, rel))
+        out = {}
+        for part, lst in ((bits[1::2], [h for h in rel if topo.die(h) == topo.die(c)]),
+                          (bits[0::2], [h for h in rel if topo.die(h) != topo.die(c)])):
+            k = len(part) // len(lst)
+            for i, h in enumerate(lst):
+                out[h] = _join(part[i * k:(i + 1) * k])
+        return out
+
+    def wmask(c):
+        return topo.mask(c, hub[c]) & ~topo.mask(c, hub[routes[c][0][0]])
+
+    def split(c):
+        far = [d for d in cores if d != c][0]
+        off = topo.mask(hub[c], far)
+        return _bits(off), _bits(topo.mask(hub[c], c) & ~off)
+
+    def order(c):
+        return sorted(range(N), key=lambda s: (when[(cores[s], c)], s))
+
+    def onward(s, c):
+        return _join(split(c)[1]) if s == order(c)[-1] else topo.mask(hub[c], c)
+
+    def landed(s, c):
+        src = cores[s]
+        snd, lst = [(x, lst) for x, lst in [(src, routes[src][0])] + routes[src][1] if c in lst][0]
+        return len(_bits(_common(topo, snd, [hub[d] for d in lst]))) // len(lst) + len(_bits(topo.mask(snd, hub[c])))
+
+    def slot(s):
+        return T.sl[:, s * N:(s + 1) * N] if s < N - 1 else T.sb[:, 3 * N:4 * N]
+
+    def turns(s):
+        return [cores[(s + 1 + i) % N] for i in range(N - 1)]
+
+    def share(s, d):
+        off, up = split(cores[s])
+        if d == cores[s]:
+            return len(up)
+        return len(off) // 4 if turns(s).index(d) < 4 else len(off) // 2
+
+    if T.rank_of(core) is None:
+        for src in cores:
+            mine = [lst for h, lst in routes[src][1] if h == core]
+            if not mine:
+                continue
+            r = cores.index(src)
+            n = len(_bits(deal(src)[core]))
+            _send(g, T, topo, core, r, [hub[d] for d in mine[0]], tot, gate=(("rs", n), ("rc", n)))
+            if core == hub[src]:
+                off, up = split(src)
+                um = _join(up)
+                rid, pid, _ = topo.addr(src)
+
+                def pass_on(s):
+                    codes, plane = _views(T, s)
+                    m = onward(s, src)
+                    g.remote_dma(plane, plane, sem["fw%d" % s], sem.ls, pid, rid, m)
+                    g.remote_dma(codes, codes, sem["fw%d" % s], sem.ls, pid, rid, m)
+                    tot["ls"] += 2 * len(_bits(m))
+
+                tot["wa"] = 2 * len(_bits(wmask(src)))
+                g.tensor.wait_ge(sem.wa, tot["wa"])
+                for s in order(src):
+                    own = s == r
+                    if own:
+                        g.tensor.wait_ge(sem.rs, n)
+                        g.tensor.wait_ge(sem.rc, n)
+                    else:
+                        tot["arr%d" % s] = landed(s, src)
+                        g.tensor.wait_ge(sem["arr%d" % s], tot["arr%d" % s])
+                    inc(g.tensor.matmul_mx(bank(s), xq(s)[0], xq(s)[1], T.wq[:], T.ws[:], True, True), "mm%d" % s)
+                    g.scalar.wait_ge(sem["mm%d" % s], 1)
+                    inc(g.scalar.activation(T.junk[:, s * NC:(s + 1) * NC], bank(s), ActivationFunctionType.Square,
+                                            scale=SH ** 0.5, accum_out=T.pa[:, N:N + 1] if own else T.pa[:, s:s + 1]),
+                        "so" if own else "sq")
+                    if own:
+                        g.vector.wait_ge(sem.so, 1)
+                        inc(g.vector.tensor_scalar(T.pa[:, r:r + 1], T.pa[:, N:N + 1], E, None, AluOpType.add), "se")
+                    elif s != order(src)[-1]:
+                        g.wait_ge(sem["arr%d" % s], tot["arr%d" % s])
+                        pass_on(s)
+                g.wait_ge(sem.sq, N - 1)
+                g.wait_ge(sem.se, 1)
+                lst = turns(r)
+                trs = [RemoteDMATransfer(dst_ids=[DstId(rid=rid, pnc=pid)], dma_engine_mask=um, remote_sem=sem.tt,
+                                         src=T.pa[:, 0:N], dst=slot(r))]
+                tot["ls"] += len(up)
+                for part, k in ((lst[:4], len(off) // 4), (lst[4:], len(off) // 2)):
+                    for i, d in enumerate(part):
+                        drid, dpid, _ = topo.addr(d)
+                        trs.append(RemoteDMATransfer(dst_ids=[DstId(rid=drid, pnc=dpid)],
+                                                     dma_engine_mask=_join(off[i * k:(i + 1) * k]), remote_sem=sem.tt,
+                                                     src=T.pa[:, 0:N], dst=slot(r)))
+                        tot["ls"] += k
+                    g.remote_dma_fused(trs, local_sem=sem.ls)
+                    trs = []
+                g.wait_ge(sem["arr%d" % order(src)[-1]], tot["arr%d" % order(src)[-1]])
+                pass_on(order(src)[-1])
+            for name in sorted(tot):
+                g.wait_ge(sem[name], tot[name])
+        return
+
+    me = cores.index(core)
+
     inc(g.sync.dma_start(T.xt[:], T.x[:]), "lx", 16)
     inc(g.sync.dma_start(T.wt[:], T.w[:]), "lw", 16)
     g.vector.wait_ge(sem.lx, 16)
@@ -191,64 +257,64 @@ def rank_program(g, core, T, topo):
     g.vector.wait_ge(sem.lw, 16)
     inc(g.vector.quantize_mx(T.wq[:], T.ws[:], T.wt[:]), "qw")
 
-    same, (near, a), (other, b) = routes[core]
-    ma, mb = halves(core, near, other)
+    same, jobs = routes[core]
+    grp = deal(core)
     codes, plane = _views(T, me)
     g.wait_ge(sem.qx, 1)
     for v, name in ((plane, "rs"), (codes, "rc")):
         trs = []
-        for h, m in ((near, ma), (other, mb)):
-            rid, pid, _ = topo.addr(h)
-            trs.append(RemoteDMATransfer(dst_ids=[DstId(rid=rid, pnc=pid)], dma_engine_mask=m, remote_sem=sem[name],
+        for h, _ in jobs:
+            rid, pid, _x = topo.addr(h)
+            trs.append(RemoteDMATransfer(dst_ids=[DstId(rid=rid, pnc=pid)], dma_engine_mask=grp[h], remote_sem=sem[name],
                                          src=v, dst=v))
-            tot["ls"] = tot.get("ls", 0) + len(_bits(m))
+            tot["ls"] = tot.get("ls", 0) + len(_bits(grp[h]))
         g.remote_dma_fused(trs, local_sem=sem.ls)
-    _send(g, T, topo, core, me, same, tot)
-
-    for s, src in enumerate(cores):
-        if s != me:
-            snd, lst = [(x, lst) for x, lst in ((src, routes[src][0]), routes[src][1], routes[src][2]) if core in lst][0]
-            tot["arr%d" % s] = len(_bits(_common(topo, snd, lst))) // len(lst) + len(_bits(topo.mask(snd, core)))
+    _send(g, T, topo, core, me, [hub[d] for d in same], tot)
+    g.wait_ge(sem.qw, 1)
+    rid, pid, _ = topo.addr(hub[core])
+    for v in (T.ws[:], T.wq[:].bitcast(dt.uint8)):
+        g.remote_dma(v, v, sem.wa, sem.ls, pid, rid, wmask(core))
+        tot["ls"] += len(_bits(wmask(core)))
 
     g.tensor.wait_ge(sem.qw, 1)
-    for s in sorted(range(N), key=lambda s: (when[(cores[s], core)], s)):
-        own = s == me
-        if own:
+    for s in order(core):
+        if s == me:
             g.tensor.wait_ge(sem.qx, 1)
         else:
-            g.tensor.wait_ge(sem["arr%d" % s], tot["arr%d" % s])
+            tot["fw%d" % s] = 2 * len(_bits(onward(s, core)))
+            g.tensor.wait_ge(sem["fw%d" % s], tot["fw%d" % s])
         inc(g.tensor.matmul_mx(bank(s), xq(s)[0], xq(s)[1], T.wq[:], T.ws[:], True, True), "mm%d" % s)
-        g.scalar.wait_ge(sem["mm%d" % s], 1)
-        inc(g.scalar.activation(T.junk[:, s * NC:(s + 1) * NC], bank(s), ActivationFunctionType.Square,
-                                scale=SH ** 0.5, accum_out=T.pa[:, N:N + 1] if own else T.pa[:, s:s + 1]),
-            "so" if own else "sq")
-        if own:
-            g.vector.wait_ge(sem.so, 1)
-            inc(g.vector.tensor_scalar(T.pa[:, me:me + 1], T.pa[:, N:N + 1], E, None, AluOpType.add), "se")
 
-    g.wait_ge(sem.sq, N - 1)
-    g.wait_ge(sem.se, 1)
-    rid, pid, _ = topo.addr(hub[core])
-    m = topo.mask(core, hub[core])
-    g.remote_dma(T.pd[me], T.pa[:, 0:N], sem.po, sem.ls, pid, rid, m)
-    tot["ls"] += len(_bits(m))
-    tot["tt"] = len(_bits(fold_mask(core)))
-
-    g.vector.wait_ge(sem.sq, N - 1)
-    g.vector.wait_ge(sem.se, 1)
-    inc(g.vector.tensor_scalar(T.a0[:, 0:N], T.pa[:, 0:N], E, None, AluOpType.add), "e1")
+    for lo, hi in ((0, me), (me + 1, N)):
+        if hi > lo:
+            inc(g.vector.memset(T.ra[:, lo:hi], 1.0 / E), "ms")
+            inc(g.vector.memset(T.cc[:, lo:hi], (SU / EPS) ** 0.5), "ms")
+    g.scalar.wait_ge(sem["mm%d" % me], 1)
+    inc(g.scalar.activation(T.junk[:, 0:NC], bank(me), ActivationFunctionType.Square, scale=SH ** 0.5,
+                            accum_out=T.pa[:, 0:1]), "so")
+    g.vector.wait_ge(sem.so, 1)
+    inc(g.vector.tensor_scalar(T.a0[:, 0:1], T.pa[:, 0:1], E, None, AluOpType.add), "e1")
     g.scalar.wait_ge(sem.e1, 1)
-    inc(g.scalar.activation(T.sa[:, 0:N], T.a0[:, 0:N], ActivationFunctionType.Sqrt, scale=KA), "e2")
+    inc(g.scalar.activation(T.sa[:, 0:1], T.a0[:, 0:1], ActivationFunctionType.Sqrt, scale=KA), "e2")
     g.vector.wait_ge(sem.e1, 1)
-    inc(g.vector.reciprocal(T.ra[:, 0:N], T.a0[:, 0:N]), "e3")
+    inc(g.vector.reciprocal(T.ra[:, me:me + 1], T.a0[:, 0:1]), "e3")
     g.vector.wait_ge(sem.e2, 1)
-    inc(g.vector.reciprocal(T.ca[:, 0:N], T.sa[:, 0:N]), "e4")
+    inc(g.vector.reciprocal(T.ca[:, 0:1], T.sa[:, 0:1]), "e4")
     g.vector.wait_ge(sem.e4, 1)
-    inc(g.vector.tensor_scalar(T.cc[:, 0:N], T.ca[:, 0:N], SH * SU ** 0.5, None, AluOpType.mult), "e5")
+    inc(g.vector.tensor_scalar(T.cc[:, me:me + 1], T.ca[:, 0:1], SH * SU ** 0.5, None, AluOpType.mult), "e5")
 
+    tot["tt"] = sum(share(s, core) for s in range(N))
+    g.vector.wait_ge(sem.ms, tot["ms"])
     g.vector.wait_ge(sem.e3, 1)
     g.vector.wait_ge(sem.e5, 1)
     g.vector.wait_ge(sem.tt, tot["tt"])
+    inc(g.vector.tensor_tensor(T.sb[:, 0:3 * N], T.sl[:, 0:3 * N], T.sl[:, 3 * N:6 * N], AluOpType.add), "a1")
+    g.vector.wait_ge(sem.a1, 1)
+    inc(g.vector.tensor_tensor(T.sd[:, 0:2 * N], T.sb[:, 0:2 * N], T.sb[:, 2 * N:4 * N], AluOpType.add), "a2")
+    g.vector.wait_ge(sem.a2, 1)
+    inc(g.vector.tensor_tensor(T.tot[:, 0:N], T.sd[:, 0:N], T.sd[:, N:2 * N], AluOpType.add), "a3")
+    g.vector.wait_ge(sem.a3, 1)
+
     inc(g.vector.tensor_tensor(T.uu[:, 0:N], T.tot[:, 0:N], T.ra[:, 0:N], AluOpType.mult), "l1")
     g.scalar.wait_ge(sem.l1, 1)
     inc(g.scalar.activation(T.su[:, 0:N], T.uu[:, 0:N], ActivationFunctionType.Sqrt, scale=SU), "fq")
@@ -256,16 +322,26 @@ def rank_program(g, core, T, topo):
     inc(g.vector.reciprocal(T.r0[:, 0:N], T.su[:, 0:N]), "fr")
     g.vector.wait_ge(sem.fr, 1)
     inc(g.vector.tensor_tensor(T.ri[:, NV:N], T.r0[:, NV:N], T.cc[:, NV:N], AluOpType.mult), "fi")
-    for j in range(NV):
-        inc(g.vector.tensor_scalar(yblk(j), bank(j), T.r0[:, j:j + 1], T.cc[:, j:j + 1], AluOpType.mult, AluOpType.mult),
-            "yv")
+    pos = {s: p for p, s in enumerate(order(core))}
+
+    def parts(lo, hi):
+        ps = [list(range(a, min(a + 2, hi))) for a in range(lo, hi, 2)]
+        return sorted(ps, key=lambda p: max(pos[j] for j in p))
+
+    for i, p in enumerate(parts(0, NV)):
+        for j in sorted(p, key=lambda j: pos[j]):
+            g.vector.wait_ge(sem["mm%d" % j], 1)
+            inc(g.vector.tensor_scalar(yblk(j), bank(j), T.r0[:, j:j + 1], T.cc[:, j:j + 1], AluOpType.mult,
+                                       AluOpType.mult), "yv%d" % i)
+        g.sync.wait_ge(sem["yv%d" % i], len(p))
+        inc(g.sync.dma_start(T.y[:, p[0] * NC:(p[-1] + 1) * NC], T.yt[:, p[0] * NC:(p[-1] + 1) * NC]), "st", 16)
     g.scalar.wait_ge(sem.fi, 1)
-    for j in range(NV, N):
-        inc(g.scalar.activation(yblk(j), bank(j), ActivationFunctionType.Copy, scale=T.ri[:, j:j + 1]), "ys")
-    g.sync.wait_ge(sem.yv, NV)
-    inc(g.sync.dma_start(T.y[:, 0:NV * NC], T.yt[:, 0:NV * NC]), "st", 16)
-    g.scalar.wait_ge(sem.ys, N - NV)
-    inc(g.scalar.dma_start(T.y[:, NV * NC:N * NC], T.yt[:, NV * NC:N * NC]), "st", 16)
+    for i, p in enumerate(parts(NV, N)):
+        for j in sorted(p, key=lambda j: pos[j]):
+            g.scalar.wait_ge(sem["mm%d" % j], 1)
+            inc(g.scalar.activation(yblk(j), bank(j), ActivationFunctionType.Copy, scale=T.ri[:, j:j + 1]), "ys%d" % i)
+        g.scalar.wait_ge(sem["ys%d" % i], len(p))
+        inc(g.scalar.dma_start(T.y[:, p[0] * NC:(p[-1] + 1) * NC], T.yt[:, p[0] * NC:(p[-1] + 1) * NC]), "st", 16)
 
     for name in sorted(tot, key=lambda s: s == "st"):
         g.wait_ge(sem[name], tot[name])

from concourse.bass import DstId, RemoteDMATransfer
from concourse.mybir import dt, AluOpType, AxisListType, ActivationFunctionType

N = 7
NC = 128
EPS = 0.001
BANK = 512
SH = 2.0 ** -20
NV = 4
KA = SH / (N * NC)
E = EPS * SH * N * NC
SU = 2.0 ** -50

SCRATCH = {
    "xt": ("sbuf", [128, 4 * NC], "bfloat16"),
    "wt": ("sbuf", [128, 4 * NC], "bfloat16"),
    "q": ("sbuf", [128, N * NC], "float8_e4m3fn_x4"),
    "sc": ("sbuf", [128, N * NC], "uint8"),
    "wq": ("sbuf", [128, NC], "float8_e4m3fn_x4"),
    "ws": ("sbuf", [128, NC], "uint8"),
    "ps": ("psum", [128, BANK * N], "float32"),
    "junk": ("sbuf", [128, N * NC], "float32"),
    "pa": ("sbuf", [128, 8], "float32"),
    "sl": ("sbuf", [128, (N - 1) * N], "float32"),
    "sb": ("sbuf", [128, 4 * N], "float32"),
    "sd": ("sbuf", [128, 2 * N], "float32"),
    "tot": ("sbuf", [128, 8], "float32"),
    "a0": ("sbuf", [128, 8], "float32"),
    "sa": ("sbuf", [128, 8], "float32"),
    "ra": ("sbuf", [128, 8], "float32"),
    "ca": ("sbuf", [128, 8], "float32"),
    "cc": ("sbuf", [128, 8], "float32"),
    "uu": ("sbuf", [128, 8], "float32"),
    "su": ("sbuf", [128, 8], "float32"),
    "r0": ("sbuf", [128, 8], "float32"),
    "ri": ("sbuf", [128, 8], "float32"),
    "yt": ("sbuf", [128, N * NC], "float32"),
}
SEMAPHORES = (["lx", "lw", "qx", "qw", "rc", "rs", "wa", "ls", "sq", "so", "se", "ms", "e1", "e2", "e3", "e4", "e5",
               "a1", "a2", "a3", "l1", "tt", "fq", "fr", "fi", "yv0", "yv1", "ys0", "ys1", "st"]
              + ["arr%d" % i for i in range(N)] + ["fw%d" % i for i in range(N)] + ["mm%d" % i for i in range(N)])


def _bits(mask):
    return [1 << i for i in range(mask.bit_length()) if (mask >> i) & 1]


def _join(bits):
    m = 0
    for b in bits:
        m |= b
    return m


def _plan(cores, topo):
    groups = []
    for c in cores:
        for grp in groups:
            if topo.same_plane(topo.chip(c), topo.chip(grp[0])):
                grp.append(c)
                break
        else:
            groups.append([c])
    groups.sort(key=lambda grp: -len(grp))
    everyone = range(topo.CHIPS * topo.CORES_PER_CHIP)
    homes = [topo.chip(c) for c in cores]
    routes, when = {}, {}
    for grp in groups:
        for i, c in enumerate(grp):
            same = grp[i + 1:] + grp[:i]
            cross = [d for d in cores if d not in grp]
            mate = [d for d in cross if topo.mates(topo.chip(c), topo.chip(d))]
            far = [d for d in cross if d not in mate]
            k = i % len(far)
            jobs = far[k:] + far[:k] + mate
            helpers = [h for h in everyone
                       if topo.chip(h) == topo.chip(c) and h not in cores
                       and all(topo.may_write(h, e) for e in everyone if topo.chip(e) in homes and e != h)]
            near = [h for h in helpers if topo.die(h) == topo.die(c)]
            other = [h for h in helpers if topo.die(h) != topo.die(c)]
            relays = [near[0], other[0], near[1], other[1]]
            while len(jobs) < len(relays) and len(same) > 2:
                jobs.append(same.pop())
            routes[c] = (same, [(h, [d]) for h, d in zip(relays, jobs)])
            when[(c, c)] = 0.0
            for p, d in enumerate(same):
                when[(c, d)] = 3.0 + p
            for d in jobs:
                when[(c, d)] = 3.5
    return routes, when


def _views(T, slot):
    lo, hi = slot * NC, (slot + 1) * NC
    return T.q[:, lo:hi].bitcast(dt.uint8), T.sc[:, lo:hi]


def _common(topo, core, dests):
    m = topo.mask(core, dests[0])
    for d in dests[1:]:
        m &= topo.mask(core, d)
    return m


def _send(g, T, topo, core, slot, dests, tot, gate=None):
    codes, plane = _views(T, slot)
    bits = _bits(_common(topo, core, dests))
    k = len(bits) // len(dests)
    if gate is not None:
        g.wait_ge(T.sem[gate[0][0]], gate[0][1])
    trs = []
    for i, d in enumerate(dests):
        rid, pid, _ = topo.addr(d)
        trs.append(RemoteDMATransfer(dst_ids=[DstId(rid=rid, pnc=pid)], dma_engine_mask=_join(bits[i * k:(i + 1) * k]),
                                     remote_sem=T.sem["arr%d" % slot], src=plane, dst=plane))
        tot["ls"] = tot.get("ls", 0) + k
    g.remote_dma_fused(trs, local_sem=T.sem.ls)
    if gate is not None:
        g.wait_ge(T.sem[gate[1][0]], gate[1][1])
    for d in dests:
        rid, pid, _ = topo.addr(d)
        m = topo.mask(core, d)
        g.remote_dma(codes, codes, T.sem["arr%d" % slot], T.sem.ls, pid, rid, m)
        tot["ls"] += len(_bits(m))


def rank_program(g, core, T, topo):
    cores = list(T.cores)
    routes, when = _plan(cores, topo)
    hub = {c: routes[c][1][0][0] for c in cores}
    sem = T.sem
    tot = {}

    def inc(ins, name, n=1):
        ins.then_inc(sem[name], n)
        tot[name] = tot.get(name, 0) + n

    def xq(s):
        return T.q[:, s * NC:(s + 1) * NC], T.sc[:, s * NC:(s + 1) * NC]

    def bank(s):
        return T.ps[:, s * BANK:s * BANK + NC]

    def yblk(s):
        return T.yt[:, s * NC:(s + 1) * NC]

    def deal(c):
        rel = [h for h, _ in routes[c][1]]
        bits = _bits(_common(topo, c, rel))
        out = {}
        for part, lst in ((bits[1::2], [h for h in rel if topo.die(h) == topo.die(c)]),
                          (bits[0::2], [h for h in rel if topo.die(h) != topo.die(c)])):
            k = len(part) // len(lst)
            for i, h in enumerate(lst):
                out[h] = _join(part[i * k:(i + 1) * k])
        return out

    def wmask(c):
        return topo.mask(c, hub[c]) & ~topo.mask(c, hub[routes[c][0][0]])

    def split(c):
        far = [d for d in cores if d != c][0]
        off = topo.mask(hub[c], far)
        return _bits(off), _bits(topo.mask(hub[c], c) & ~off)

    def order(c):
        return sorted(range(N), key=lambda s: (when[(cores[s], c)], s))

    def onward(s, c):
        return _join(split(c)[1]) if s == order(c)[-1] else topo.mask(hub[c], c)

    def landed(s, c):
        src = cores[s]
        snd, lst = [(x, lst) for x, lst in [(src, routes[src][0])] + routes[src][1] if c in lst][0]
        return len(_bits(_common(topo, snd, [hub[d] for d in lst]))) // len(lst) + len(_bits(topo.mask(snd, hub[c])))

    def slot(s):
        return T.sl[:, s * N:(s + 1) * N] if s < N - 1 else T.sb[:, 3 * N:4 * N]

    def turns(s):
        return [cores[(s + 1 + i) % N] for i in range(N - 1)]

    def share(s, d):
        off, up = split(cores[s])
        if d == cores[s]:
            return len(up)
        return len(off) // 4 if turns(s).index(d) < 4 else len(off) // 2

    if T.rank_of(core) is None:
        for src in cores:
            mine = [lst for h, lst in routes[src][1] if h == core]
            if not mine:
                continue
            r = cores.index(src)
            n = len(_bits(deal(src)[core]))
            _send(g, T, topo, core, r, [hub[d] for d in mine[0]], tot, gate=(("rs", n), ("rc", n)))
            if core == hub[src]:
                off, up = split(src)
                um = _join(up)
                rid, pid, _ = topo.addr(src)

                def pass_on(s):
                    codes, plane = _views(T, s)
                    m = onward(s, src)
                    g.remote_dma(plane, plane, sem["fw%d" % s], sem.ls, pid, rid, m)
                    g.remote_dma(codes, codes, sem["fw%d" % s], sem.ls, pid, rid, m)
                    tot["ls"] += 2 * len(_bits(m))

                tot["wa"] = 2 * len(_bits(wmask(src)))
                g.tensor.wait_ge(sem.wa, tot["wa"])
                for s in order(src):
                    own = s == r
                    if own:
                        g.tensor.wait_ge(sem.rs, n)
                        g.tensor.wait_ge(sem.rc, n)
                    else:
                        tot["arr%d" % s] = landed(s, src)
                        g.tensor.wait_ge(sem["arr%d" % s], tot["arr%d" % s])
                    inc(g.tensor.matmul_mx(bank(s), xq(s)[0], xq(s)[1], T.wq[:], T.ws[:], True, True), "mm%d" % s)
                    g.scalar.wait_ge(sem["mm%d" % s], 1)
                    inc(g.scalar.activation(T.junk[:, s * NC:(s + 1) * NC], bank(s), ActivationFunctionType.Square,
                                            scale=SH ** 0.5, accum_out=T.pa[:, N:N + 1] if own else T.pa[:, s:s + 1]),
                        "so" if own else "sq")
                    if own:
                        g.vector.wait_ge(sem.so, 1)
                        inc(g.vector.tensor_scalar(T.pa[:, r:r + 1], T.pa[:, N:N + 1], E, None, AluOpType.add), "se")
                    elif s != order(src)[-1]:
                        g.wait_ge(sem["arr%d" % s], tot["arr%d" % s])
                        pass_on(s)
                g.wait_ge(sem.sq, N - 1)
                g.wait_ge(sem.se, 1)
                lst = turns(r)
                trs = [RemoteDMATransfer(dst_ids=[DstId(rid=rid, pnc=pid)], dma_engine_mask=um, remote_sem=sem.tt,
                                         src=T.pa[:, 0:N], dst=slot(r))]
                tot["ls"] += len(up)
                for part, k in ((lst[:4], len(off) // 4), (lst[4:], len(off) // 2)):
                    for i, d in enumerate(part):
                        drid, dpid, _ = topo.addr(d)
                        trs.append(RemoteDMATransfer(dst_ids=[DstId(rid=drid, pnc=dpid)],
                                                     dma_engine_mask=_join(off[i * k:(i + 1) * k]), remote_sem=sem.tt,
                                                     src=T.pa[:, 0:N], dst=slot(r)))
                        tot["ls"] += k
                    g.remote_dma_fused(trs, local_sem=sem.ls)
                    trs = []
                g.wait_ge(sem["arr%d" % order(src)[-1]], tot["arr%d" % order(src)[-1]])
                pass_on(order(src)[-1])
            for name in sorted(tot):
                g.wait_ge(sem[name], tot[name])
        return

    me = cores.index(core)

    inc(g.sync.dma_start(T.xt[:], T.x[:]), "lx", 16)
    inc(g.sync.dma_start(T.wt[:], T.w[:]), "lw", 16)
    g.vector.wait_ge(sem.lx, 16)
    inc(g.vector.quantize_mx(xq(me)[0], xq(me)[1], T.xt[:]), "qx")
    g.vector.wait_ge(sem.lw, 16)
    inc(g.vector.quantize_mx(T.wq[:], T.ws[:], T.wt[:]), "qw")

    same, jobs = routes[core]
    grp = deal(core)
    codes, plane = _views(T, me)
    g.wait_ge(sem.qx, 1)
    for v, name in ((plane, "rs"), (codes, "rc")):
        trs = []
        for h, _ in jobs:
            rid, pid, _x = topo.addr(h)
            trs.append(RemoteDMATransfer(dst_ids=[DstId(rid=rid, pnc=pid)], dma_engine_mask=grp[h], remote_sem=sem[name],
                                         src=v, dst=v))
            tot["ls"] = tot.get("ls", 0) + len(_bits(grp[h]))
        g.remote_dma_fused(trs, local_sem=sem.ls)
    _send(g, T, topo, core, me, [hub[d] for d in same], tot)
    g.wait_ge(sem.qw, 1)
    rid, pid, _ = topo.addr(hub[core])
    for v in (T.ws[:], T.wq[:].bitcast(dt.uint8)):
        g.remote_dma(v, v, sem.wa, sem.ls, pid, rid, wmask(core))
        tot["ls"] += len(_bits(wmask(core)))

    g.tensor.wait_ge(sem.qw, 1)
    for s in order(core):
        if s == me:
            g.tensor.wait_ge(sem.qx, 1)
        else:
            tot["fw%d" % s] = 2 * len(_bits(onward(s, core)))
            g.tensor.wait_ge(sem["fw%d" % s], tot["fw%d" % s])
        inc(g.tensor.matmul_mx(bank(s), xq(s)[0], xq(s)[1], T.wq[:], T.ws[:], True, True), "mm%d" % s)

    for lo, hi in ((0, me), (me + 1, N)):
        if hi > lo:
            inc(g.vector.memset(T.ra[:, lo:hi], 1.0 / E), "ms")
            inc(g.vector.memset(T.cc[:, lo:hi], (SU / EPS) ** 0.5), "ms")
    g.scalar.wait_ge(sem["mm%d" % me], 1)
    inc(g.scalar.activation(T.junk[:, 0:NC], bank(me), ActivationFunctionType.Square, scale=SH ** 0.5,
                            accum_out=T.pa[:, 0:1]), "so")
    g.vector.wait_ge(sem.so, 1)
    inc(g.vector.tensor_scalar(T.a0[:, 0:1], T.pa[:, 0:1], E, None, AluOpType.add), "e1")
    g.scalar.wait_ge(sem.e1, 1)
    inc(g.scalar.activation(T.sa[:, 0:1], T.a0[:, 0:1], ActivationFunctionType.Sqrt, scale=KA), "e2")
    g.vector.wait_ge(sem.e1, 1)
    inc(g.vector.reciprocal(T.ra[:, me:me + 1], T.a0[:, 0:1]), "e3")
    g.vector.wait_ge(sem.e2, 1)
    inc(g.vector.reciprocal(T.ca[:, 0:1], T.sa[:, 0:1]), "e4")
    g.vector.wait_ge(sem.e4, 1)
    inc(g.vector.tensor_scalar(T.cc[:, me:me + 1], T.ca[:, 0:1], SH * SU ** 0.5, None, AluOpType.mult), "e5")

    tot["tt"] = sum(share(s, core) for s in range(N))
    g.vector.wait_ge(sem.ms, tot["ms"])
    g.vector.wait_ge(sem.e3, 1)
    g.vector.wait_ge(sem.e5, 1)
    g.vector.wait_ge(sem.tt, tot["tt"])
    inc(g.vector.tensor_tensor(T.sb[:, 0:3 * N], T.sl[:, 0:3 * N], T.sl[:, 3 * N:6 * N], AluOpType.add), "a1")
    g.vector.wait_ge(sem.a1, 1)
    inc(g.vector.tensor_tensor(T.sd[:, 0:2 * N], T.sb[:, 0:2 * N], T.sb[:, 2 * N:4 * N], AluOpType.add), "a2")
    g.vector.wait_ge(sem.a2, 1)
    inc(g.vector.tensor_tensor(T.tot[:, 0:N], T.sd[:, 0:N], T.sd[:, N:2 * N], AluOpType.add), "a3")
    g.vector.wait_ge(sem.a3, 1)

    inc(g.vector.tensor_tensor(T.uu[:, 0:N], T.tot[:, 0:N], T.ra[:, 0:N], AluOpType.mult), "l1")
    g.scalar.wait_ge(sem.l1, 1)
    inc(g.scalar.activation(T.su[:, 0:N], T.uu[:, 0:N], ActivationFunctionType.Sqrt, scale=SU), "fq")
    g.vector.wait_ge(sem.fq, 1)
    inc(g.vector.reciprocal(T.r0[:, 0:N], T.su[:, 0:N]), "fr")
    g.vector.wait_ge(sem.fr, 1)
    inc(g.vector.tensor_tensor(T.ri[:, NV:N], T.r0[:, NV:N], T.cc[:, NV:N], AluOpType.mult), "fi")
    pos = {s: p for p, s in enumerate(order(core))}

    def parts(lo, hi):
        ps = [list(range(a, min(a + 2, hi))) for a in range(lo, hi, 2)]
        return sorted(ps, key=lambda p: max(pos[j] for j in p))

    for i, p in enumerate(parts(0, NV)):
        for j in sorted(p, key=lambda j: pos[j]):
            g.vector.wait_ge(sem["mm%d" % j], 1)
            inc(g.vector.tensor_scalar(yblk(j), bank(j), T.r0[:, j:j + 1], T.cc[:, j:j + 1], AluOpType.mult,
                                       AluOpType.mult), "yv%d" % i)
        g.sync.wait_ge(sem["yv%d" % i], len(p))
        inc(g.sync.dma_start(T.y[:, p[0] * NC:(p[-1] + 1) * NC], T.yt[:, p[0] * NC:(p[-1] + 1) * NC]), "st", 16)
    g.scalar.wait_ge(sem.fi, 1)
    for i, p in enumerate(parts(NV, N)):
        for j in sorted(p, key=lambda j: pos[j]):
            g.scalar.wait_ge(sem["mm%d" % j], 1)
            inc(g.scalar.activation(yblk(j), bank(j), ActivationFunctionType.Copy, scale=T.ri[:, j:j + 1]), "ys%d" % i)
        g.scalar.wait_ge(sem["ys%d" % i], len(p))
        inc(g.scalar.dma_start(T.y[:, p[0] * NC:(p[-1] + 1) * NC], T.yt[:, p[0] * NC:(p[-1] + 1) * NC]), "st", 16)

    for name in sorted(tot, key=lambda s: s == "st"):
        g.wait_ge(sem[name], tot[name])
